import numpy as np
import ml_dtypes


def mxq(x, axis, fmt="e4m3"):
    dtype, down = {"e4m3": (ml_dtypes.float8_e4m3fn, 7), "e5m2": (ml_dtypes.float8_e5m2, 14)}[fmt]
    v = np.moveaxis(np.asarray(x, np.float32).astype(ml_dtypes.bfloat16).astype(np.float64), axis, -1)
    blocks = v.reshape(v.shape[:-1] + (-1, 32))
    amax = np.abs(blocks).max(-1, keepdims=True)
    byte = np.maximum(np.where(amax > 0, np.frexp(amax)[1] - 1 + 127, 0) - down, 1)
    scale = np.exp2(byte - 127.0)
    codes = (blocks / scale).astype(np.float32).astype(dtype).astype(np.float64)
    return np.moveaxis((codes * scale).reshape(v.shape), -1, axis)


WIDE = False


def mx_kscale(k):
    if not WIDE:
        return np.ones(k)
    levels = np.array([30, -30])
    if k % 512:
        return np.exp2(np.random.permutation(np.resize(levels, k // 32))).repeat(32)
    a = np.empty((k // 512, 16))
    for p in range(k // 512):
        a[p, :8] = np.random.permutation(np.resize(levels, 8))
        for g in range(8):
            far = levels[np.abs(levels - a[p, g]) >= 10]
            a[p, g + 8] = far[np.random.randint(len(far))]
    return np.exp2(a.ravel()).repeat(32)


def f64(x):
    return np.asarray(x).astype(np.float64)


K, M, T = 512, 1536, 2048


def setup_inputs():
    n = np.random.standard_normal
    s1 = mx_kscale(K)[:, None]
    s2 = mx_kscale(K)[:, None]
    return {
        "w": (n((K, M)) / np.sqrt(K) * s1).astype(np.float32),
        "xd": (n((K, T)) / s1).astype(np.float32),
        "wd": (n((K, M)) / np.sqrt(K) * s2).astype(np.float32),
        "x": (n((K, T)) / s2).astype(np.float32),
        "b": (0.3 * n(1536)).astype(np.float32),
    }


def reference(w, xd, wd, x, b):
    w_ = mxq(f64(w), 0, "e4m3")
    xd_ = mxq(f64(xd), 0, "e5m2")
    wd_ = mxq(f64(wd), 0, "e5m2")
    x_ = mxq(f64(x), 0, "e4m3")
    y = xd_.T @ w_ + x_.T @ wd_
    return y + f64(b)[None, :]

@@ -1,0 +1,177 @@
+from contextlib import ExitStack
+
+import concourse.mybir as mybir
+from concourse.masks import make_identity
+
+K, M, T = 512, 1536, 2048
+FLOPS = 2 * 2 * K * M * T
+
+F32 = mybir.dt.float32
+BF16 = mybir.dt.bfloat16
+U32 = mybir.dt.uint32
+U8 = mybir.dt.uint8
+E4M3 = mybir.dt.float8_e4m3fn_x4
+E5M2 = mybir.dt.float8_e5m2_x4
+ADD = mybir.AluOpType.add
+
+P = 128
+PACK = 4
+CHUNK = 512
+N_TILES = M // CHUNK
+
+FORMAT = {"w": E4M3, "x": E4M3, "xd": E5M2, "wd": E5M2}
+WIDTH = {"w": M, "wd": M, "x": T, "xd": T}
+
+LOADS = [
+    ("w", 0, 512), ("xd", 0, 512), ("wd", 0, 512), ("x", 0, 512),
+    ("w", 512, 512), ("wd", 512, 512), ("w", 1024, 512), ("wd", 1024, 512),
+    ("xd", 512, 512), ("x", 512, 512),
+    ("xd", 1024, 512), ("x", 1024, 512), ("xd", 1536, 512), ("x", 1536, 512),
+]
+ON_VECTOR = {("w", 0), ("wd", 0), ("w", 512)}
+GROUPS_A_STEP = 6
+
+
+def tile_mix_jvp_tm_bias_kernel(tc, w, xd, wd, x, b, out):
+    nc = tc.nc
+    dram = {"w": w, "xd": xd, "wd": wd, "x": x}
+
+    with ExitStack() as ctx:
+        keep = ctx.enter_context(tc.tile_pool(name="keep", bufs=1))
+        stage = ctx.enter_context(tc.tile_pool(name="stage", bufs=4))
+        results = ctx.enter_context(tc.tile_pool(name="results", bufs=9))
+        psum = ctx.enter_context(tc.psum_pool(name="psum", bufs=8))
+        ctx.enter_context(tc.manual_schedule())
+
+        codes = {}
+        scales = {}
+        for key in WIDTH:
+            codes[key] = keep.tile([P, WIDTH[key]], U32, align_bytes=64, name="codes_" + key)
+            scales[key] = keep.tile([P, WIDTH[key]], U8, align_bytes=64, name="scales_" + key)
+
+        per_part = M // P
+        b_cols = keep.tile([P, per_part], F32, name="b_cols")
+        nc.scalar.dma_start(out=b_cols[:], in_=b.rearrange("(p c) -> p c", c=per_part))
+
+        source = {}
+        chunks = []
+        for key, first, cols in LOADS:
+            raw = keep.tile([P, PACK, cols], F32, name="raw_%s_%d" % (key, first))
+            nc.sync.dma_start(
+                out=raw[:],
+                in_=dram[key].rearrange("(p j) c -> p j c", j=PACK)[:, :, first : first + cols],
+            )
+            for c0 in range(0, cols, CHUNK):
+                source[(key, first + c0)] = raw[:, :, c0 : c0 + CHUNK]
+                chunks.append((key, first + c0))
+
+        identity = keep.tile([P, P], F32, name="identity")
+        make_identity(nc, identity[:])
+        bias = keep.tile([P, M], F32, name="bias")
+
+        def spread_bias():
+            for g in range(per_part // 4):
+                bank = psum.tile([P, CHUNK], F32, name="acc")
+                for i in range(4):
+                    c = 4 * g + i
+                    nc.tensor.transpose(
+                        bank[:, i * P : (i + 1) * P],
+                        b_cols[:, c : c + 1].to_broadcast([P, P]),
+                        identity[:],
+                    )
+                nc.vector.tensor_copy(
+                    out=bias[:].rearrange("p (q c) -> p q c", c=per_part)[:, :, 4 * g : 4 * g + 4],
+                    in_=bank[:].rearrange("p (c q) -> p q c", c=4),
+                )
+
+        grouped = {}
+
+        def interleave(chunk):
+            tile = stage.tile([P, CHUNK, PACK], BF16, align_bytes=64, name="grouped")
+            grouped[chunk] = tile
+            view = source[chunk].rearrange("p j c -> p c j")
+            if chunk in ON_VECTOR:
+                nc.vector.tensor_copy(out=tile[:], in_=view)
+            else:
+                nc.scalar.copy(out=tile[:], in_=view)
+
+        def quantize(chunk):
+            key, first = chunk
+            cols = slice(first, first + CHUNK)
+            nc.vector.quantize_mx(
+                out=codes[key][:, cols].bitcast(FORMAT[key]),
+                scales=scales[key][:, cols],
+                in_=grouped[chunk][:].rearrange("p c j -> p (c j)"),
+            )
+
+        banks = {}
+        rows = {}
+
+        def multiply(group):
+            t, n = group
+            t_cols = slice(t * P, (t + 1) * P)
+            n_cols = slice(n * CHUNK, (n + 1) * CHUNK)
+            acc = psum.tile([P, CHUNK], F32, name="acc")
+            banks[group] = acc
+            for still, moving in (("xd", "w"), ("x", "wd")):
+                nc.tensor.matmul_mx(
+                    out=acc[:],
+                    lhsT=codes[still][:, t_cols].bitcast(FORMAT[still]),
+                    lhsT_scale=scales[still][:, t_cols],
+                    rhs=codes[moving][:, n_cols].bitcast(FORMAT[moving]),
+                    rhs_scale=scales[moving][:, n_cols],
+                    start=(still == "xd"),
+                    stop=(still == "x"),
+                )
+
+        def finish(group):
+            t, n = group
+            n_cols = slice(n * CHUNK, (n + 1) * CHUNK)
+            if n == 0:
+                row = results.tile([P, M], F32, name="row")
+                rows[t] = row
+            nc.vector.tensor_tensor(
+                out=rows[t][:, n_cols], in0=banks[group][:], in1=bias[:, n_cols], op=ADD
+            )
+            if n == N_TILES - 1:
+                nc.sync.dma_start(out=out[t * P : (t + 1) * P, :], in_=rows[t][:])
+
+        done = set()
+        issued = set()
+
+        def newly_ready():
+            ready = []
+            for t4 in range(0, T // P, 4):
+                for n in range(N_TILES):
+                    need = [("xd", t4 * P), ("x", t4 * P), ("w", n * CHUNK), ("wd", n * CHUNK)]
+                    if all([c in done for c in need]):
+                        for t in range(t4, t4 + 4):
+                            if (t, n) not in issued:
+                                ready.append((t, n))
+                                issued.add((t, n))
+            if len(done) > 8:
+                ready = sorted(ready)
+            return ready
+
+        waiting = []
+        in_psum = []
+        step = 0
+        while step <= len(chunks) or waiting or in_psum:
+            if step < len(chunks):
+                interleave(chunks[step])
+            if 1 <= step <= len(chunks):
+                quantize(chunks[step - 1])
+                done.add(chunks[step - 1])
+                waiting.extend(newly_ready())
+            if step == 1:
+                spread_bias()
+            old = in_psum
+            new = waiting[:GROUPS_A_STEP]
+            waiting = waiting[GROUPS_A_STEP:]
+            in_psum = new
+            for i in range(max(len(old), len(new))):
+                if i < len(old):
+                    finish(old[i])
+                if i < len(new):
+                    multiply(new[i])
+            step += 1

@@ -23,12 +23,11 @@ FORMAT = {"w": E4M3, "x": E4M3, "xd": E5M2, "wd": E5M2}
 WIDTH = {"w": M, "wd": M, "x": T, "xd": T}
 
 LOADS = [
-    ("w", 0, 512), ("xd", 0, 512), ("wd", 0, 512), ("x", 0, 512),
-    ("w", 512, 512), ("wd", 512, 512), ("w", 1024, 512), ("wd", 1024, 512),
-    ("xd", 512, 512), ("x", 512, 512),
-    ("xd", 1024, 512), ("x", 1024, 512), ("xd", 1536, 512), ("x", 1536, 512),
+    ("w", 0, 1536), ("wd", 0, 1536),
+    ("xd", 0, 512), ("x", 0, 512), ("xd", 512, 512), ("x", 512, 512),
+    ("xd", 1024, 1024), ("x", 1024, 1024),
 ]
-ON_VECTOR = {("w", 0), ("wd", 0), ("w", 512)}
+ON_VECTOR = {("w", 0), ("w", 1024), ("wd", 0), ("wd", 1024)}
 GROUPS_A_STEP = 6
 
 
@@ -149,9 +148,7 @@ def tile_mix_jvp_tm_bias_kernel(tc, w, xd, wd, x, b, out):
                             if (t, n) not in issued:
                                 ready.append((t, n))
                                 issued.add((t, n))
-            if len(done) > 8:
-                ready = sorted(ready)
-            return ready
+            return sorted(ready)
 
         waiting = []
         in_psum = []

@@ -23,12 +23,37 @@ FORMAT = {"w": E4M3, "x": E4M3, "xd": E5M2, "wd": E5M2}
 WIDTH = {"w": M, "wd": M, "x": T, "xd": T}
 
 LOADS = [
-    ("w", 0, 1536), ("wd", 0, 1536),
-    ("xd", 0, 512), ("x", 0, 512), ("xd", 512, 512), ("x", 512, 512),
-    ("xd", 1024, 1024), ("x", 1024, 1024),
+    ("w", 0, 1536),
+    ("xd", 0, 512),
+    ("x", 0, 512),
+    ("wd", 0, 1024),
+    ("wd", 1024, 512),
+    ("xd", 512, 512),
+    ("x", 512, 512),
+    ("xd", 1024, 512),
+    ("x", 1024, 512),
+    ("xd", 1536, 512),
+    ("x", 1536, 512),
 ]
-ON_VECTOR = {("w", 0), ("w", 1024), ("wd", 0), ("wd", 1024)}
+CHUNKS = [
+    ("w", 0),
+    ("w", 512),
+    ("xd", 0),
+    ("w", 1024),
+    ("x", 0),
+    ("wd", 0),
+    ("wd", 512),
+    ("wd", 1024),
+    ("xd", 512),
+    ("x", 512),
+    ("xd", 1024),
+    ("x", 1024),
+    ("xd", 1536),
+    ("x", 1536),
+]
+ON_VECTOR = {("w", 0), ("w", 512), ("w", 1024), ("wd", 0)}
 GROUPS_A_STEP = 6
+PAIR = 2
 
 
 def tile_mix_jvp_tm_bias_kernel(tc, w, xd, wd, x, b, out):
@@ -37,8 +62,8 @@ def tile_mix_jvp_tm_bias_kernel(tc, w, xd, wd, x, b, out):
 
     with ExitStack() as ctx:
         keep = ctx.enter_context(tc.tile_pool(name="keep", bufs=1))
-        stage = ctx.enter_context(tc.tile_pool(name="stage", bufs=4))
-        results = ctx.enter_context(tc.tile_pool(name="results", bufs=9))
+        stage = ctx.enter_context(tc.tile_pool(name="stage", bufs=3))
+        results = ctx.enter_context(tc.tile_pool(name="results", bufs=5))
         psum = ctx.enter_context(tc.psum_pool(name="psum", bufs=8))
         ctx.enter_context(tc.manual_schedule())
 
@@ -53,7 +78,6 @@ def tile_mix_jvp_tm_bias_kernel(tc, w, xd, wd, x, b, out):
         nc.scalar.dma_start(out=b_cols[:], in_=b.rearrange("(p c) -> p c", c=per_part))
 
         source = {}
-        chunks = []
         for key, first, cols in LOADS:
             raw = keep.tile([P, PACK, cols], F32, name="raw_%s_%d" % (key, first))
             nc.sync.dma_start(
@@ -62,7 +86,6 @@ def tile_mix_jvp_tm_bias_kernel(tc, w, xd, wd, x, b, out):
             )
             for c0 in range(0, cols, CHUNK):
                 source[(key, first + c0)] = raw[:, :, c0 : c0 + CHUNK]
-                chunks.append((key, first + c0))
 
         identity = keep.tile([P, P], F32, name="identity")
         make_identity(nc, identity[:])
@@ -78,10 +101,12 @@ def tile_mix_jvp_tm_bias_kernel(tc, w, xd, wd, x, b, out):
                         b_cols[:, c : c + 1].to_broadcast([P, P]),
                         identity[:],
                     )
-                nc.vector.tensor_copy(
+                nc.scalar.copy(
                     out=bias[:].rearrange("p (q c) -> p q c", c=per_part)[:, :, 4 * g : 4 * g + 4],
                     in_=bank[:].rearrange("p (c q) -> p q c", c=4),
                 )
+
+        spread_bias()
 
         grouped = {}
 
@@ -89,10 +114,14 @@ def tile_mix_jvp_tm_bias_kernel(tc, w, xd, wd, x, b, out):
             tile = stage.tile([P, CHUNK, PACK], BF16, align_bytes=64, name="grouped")
             grouped[chunk] = tile
             view = source[chunk].rearrange("p j c -> p c j")
+            target = tile[:]
+            if chunk[0] in ("x", "xd"):
+                view = source[chunk].rearrange("p j (m s) -> p s m j", s=PAIR)
+                target = tile[:].rearrange("p (s m) j -> p s m j", s=PAIR)
             if chunk in ON_VECTOR:
-                nc.vector.tensor_copy(out=tile[:], in_=view)
+                nc.vector.tensor_copy(out=target, in_=view)
             else:
-                nc.scalar.copy(out=tile[:], in_=view)
+                nc.scalar.copy(out=target, in_=view)
 
         def quantize(chunk):
             key, first = chunk
@@ -107,8 +136,9 @@ def tile_mix_jvp_tm_bias_kernel(tc, w, xd, wd, x, b, out):
         rows = {}
 
         def multiply(group):
-            t, n = group
-            t_cols = slice(t * P, (t + 1) * P)
+            pair, s, n = group
+            t_first = (pair // 2) * CHUNK + s * (CHUNK // PAIR) + (pair % 2) * P
+            t_cols = slice(t_first, t_first + P)
             n_cols = slice(n * CHUNK, (n + 1) * CHUNK)
             acc = psum.tile([P, CHUNK], F32, name="acc")
             banks[group] = acc
@@ -123,45 +153,43 @@ def tile_mix_jvp_tm_bias_kernel(tc, w, xd, wd, x, b, out):
                     stop=(still == "x"),
                 )
 
+        last_pair = T // (PAIR * P) - 1
+
         def finish(group):
-            t, n = group
+            pair, s, n = group
             n_cols = slice(n * CHUNK, (n + 1) * CHUNK)
-            if n == 0:
-                row = results.tile([P, M], F32, name="row")
-                rows[t] = row
+            if pair not in rows:
+                row = results.tile([P, PAIR, M], F32, name="row")
+                rows[pair] = row
             nc.vector.tensor_tensor(
-                out=rows[t][:, n_cols], in0=banks[group][:], in1=bias[:, n_cols], op=ADD
+                out=rows[pair][:, s, n_cols], in0=banks[group][:], in1=bias[:, n_cols], op=ADD
             )
             if n == N_TILES - 1:
-                nc.sync.dma_start(out=out[t * P : (t + 1) * P, :], in_=rows[t][:])
+                target = out[pair * PAIR * P : (pair + 1) * PAIR * P, :].rearrange("(m s) c -> m s c", s=PAIR)
+                if pair == last_pair:
+                    nc.sync.dma_start(out=target[:, s, :], in_=rows[pair][:, s, :])
+                elif s == PAIR - 1:
+                    nc.sync.dma_start(out=target, in_=rows[pair][:])
 
         done = set()
         issued = set()
 
         def newly_ready():
             ready = []
-            for t4 in range(0, T // P, 4):
-                for n in range(N_TILES):
-                    need = [("xd", t4 * P), ("x", t4 * P), ("w", n * CHUNK), ("wd", n * CHUNK)]
-                    if all([c in done for c in need]):
-                        for t in range(t4, t4 + 4):
-                            if (t, n) not in issued:
-                                ready.append((t, n))
-                                issued.add((t, n))
-            return sorted(ready)
+            for pair in range(T // (PAIR * P)):
+                for s in range(PAIR):
+                    for n in range(N_TILES):
+                        t_first = (pair // 2) * CHUNK
+                        need = [("xd", t_first), ("x", t_first), ("w", n * CHUNK), ("wd", n * CHUNK)]
+                        if all([c in done for c in need]) and (pair, s, n) not in issued:
+                            ready.append((pair, s, n))
+                            issued.add((pair, s, n))
+            return ready
 
         waiting = []
         in_psum = []
         step = 0
-        while step <= len(chunks) or waiting or in_psum:
-            if step < len(chunks):
-                interleave(chunks[step])
-            if 1 <= step <= len(chunks):
-                quantize(chunks[step - 1])
-                done.add(chunks[step - 1])
-                waiting.extend(newly_ready())
-            if step == 1:
-                spread_bias()
+        while step <= len(CHUNKS) or waiting or in_psum:
             old = in_psum
             new = waiting[:GROUPS_A_STEP]
             waiting = waiting[GROUPS_A_STEP:]
@@ -171,4 +199,10 @@ def tile_mix_jvp_tm_bias_kernel(tc, w, xd, wd, x, b, out):
                     finish(old[i])
                 if i < len(new):
                     multiply(new[i])
+            if 1 <= step <= len(CHUNKS):
+                quantize(CHUNKS[step - 1])
+                done.add(CHUNKS[step - 1])
+                waiting = sorted(waiting + newly_ready())
+            if step < len(CHUNKS):
+                interleave(CHUNKS[step])
             step += 1

@@ -23,37 +23,38 @@ FORMAT = {"w": E4M3, "x": E4M3, "xd": E5M2, "wd": E5M2}
 WIDTH = {"w": M, "wd": M, "x": T, "xd": T}
 
 LOADS = [
-    ("w", 0, 1536),
-    ("xd", 0, 512),
-    ("x", 0, 512),
+    ("w", 0, 1024),
     ("wd", 0, 1024),
+    ("x", 0, 512),
+    ("xd", 0, 512),
+    ("w", 1024, 512),
     ("wd", 1024, 512),
-    ("xd", 512, 512),
     ("x", 512, 512),
-    ("xd", 1024, 512),
-    ("x", 1024, 512),
-    ("xd", 1536, 512),
-    ("x", 1536, 512),
+    ("xd", 512, 512),
+    ("xd", 1024, 1024),
+    ("x", 1024, 1024),
 ]
 CHUNKS = [
     ("w", 0),
     ("w", 512),
-    ("xd", 0),
-    ("w", 1024),
-    ("x", 0),
     ("wd", 0),
     ("wd", 512),
+    ("x", 0),
+    ("xd", 0),
+    ("w", 1024),
     ("wd", 1024),
-    ("xd", 512),
     ("x", 512),
+    ("xd", 512),
     ("xd", 1024),
-    ("x", 1024),
     ("xd", 1536),
+    ("x", 1024),
     ("x", 1536),
 ]
-ON_VECTOR = {("w", 0), ("w", 512), ("w", 1024), ("wd", 0)}
-GROUPS_A_STEP = 6
+ON_VECTOR = {("w", 0), ("wd", 0), ("xd", 0)}
+GROUPS_A_STEP = 8
 PAIR = 2
+FIRST_SPLIT = 5
+LAG = 2
 
 
 def tile_mix_jvp_tm_bias_kernel(tc, w, xd, wd, x, b, out):
@@ -62,7 +63,7 @@ def tile_mix_jvp_tm_bias_kernel(tc, w, xd, wd, x, b, out):
 
     with ExitStack() as ctx:
         keep = ctx.enter_context(tc.tile_pool(name="keep", bufs=1))
-        stage = ctx.enter_context(tc.tile_pool(name="stage", bufs=3))
+        stage = ctx.enter_context(tc.tile_pool(name="stage", bufs=4))
         results = ctx.enter_context(tc.tile_pool(name="results", bufs=5))
         psum = ctx.enter_context(tc.psum_pool(name="psum", bufs=8))
         ctx.enter_context(tc.manual_schedule())
@@ -114,14 +115,10 @@ def tile_mix_jvp_tm_bias_kernel(tc, w, xd, wd, x, b, out):
             tile = stage.tile([P, CHUNK, PACK], BF16, align_bytes=64, name="grouped")
             grouped[chunk] = tile
             view = source[chunk].rearrange("p j c -> p c j")
-            target = tile[:]
-            if chunk[0] in ("x", "xd"):
-                view = source[chunk].rearrange("p j (m s) -> p s m j", s=PAIR)
-                target = tile[:].rearrange("p (s m) j -> p s m j", s=PAIR)
             if chunk in ON_VECTOR:
-                nc.vector.tensor_copy(out=target, in_=view)
+                nc.vector.tensor_copy(out=tile[:], in_=view)
             else:
-                nc.scalar.copy(out=target, in_=view)
+                nc.scalar.copy(out=tile[:], in_=view)
 
         def quantize(chunk):
             key, first = chunk
@@ -137,7 +134,7 @@ def tile_mix_jvp_tm_bias_kernel(tc, w, xd, wd, x, b, out):
 
         def multiply(group):
             pair, s, n = group
-            t_first = (pair // 2) * CHUNK + s * (CHUNK // PAIR) + (pair % 2) * P
+            t_first = (pair * PAIR + s) * P
             t_cols = slice(t_first, t_first + P)
             n_cols = slice(n * CHUNK, (n + 1) * CHUNK)
             acc = psum.tile([P, CHUNK], F32, name="acc")
@@ -153,8 +150,6 @@ def tile_mix_jvp_tm_bias_kernel(tc, w, xd, wd, x, b, out):
                     stop=(still == "x"),
                 )
 
-        last_pair = T // (PAIR * P) - 1
-
         def finish(group):
             pair, s, n = group
             n_cols = slice(n * CHUNK, (n + 1) * CHUNK)
@@ -165,11 +160,13 @@ def tile_mix_jvp_tm_bias_kernel(tc, w, xd, wd, x, b, out):
                 out=rows[pair][:, s, n_cols], in0=banks[group][:], in1=bias[:, n_cols], op=ADD
             )
             if n == N_TILES - 1:
-                target = out[pair * PAIR * P : (pair + 1) * PAIR * P, :].rearrange("(m s) c -> m s c", s=PAIR)
-                if pair == last_pair:
-                    nc.sync.dma_start(out=target[:, s, :], in_=rows[pair][:, s, :])
+                target = out[pair * PAIR * P : (pair + 1) * PAIR * P, :].rearrange("(s m) c -> m s c", s=PAIR)
+                if pair >= FIRST_SPLIT:
+                    queue = nc.scalar if s == PAIR - 1 else nc.sync
+                    queue.dma_start(out=target[:, s, :], in_=rows[pair][:, s, :])
                 elif s == PAIR - 1:
-                    nc.sync.dma_start(out=target, in_=rows[pair][:])
+                    queue = nc.scalar if pair == FIRST_SPLIT - 1 else nc.sync
+                    queue.dma_start(out=target, in_=rows[pair][:])
 
         done = set()
         issued = set()
@@ -189,20 +186,21 @@ def tile_mix_jvp_tm_bias_kernel(tc, w, xd, wd, x, b, out):
         waiting = []
         in_psum = []
         step = 0
-        while step <= len(CHUNKS) or waiting or in_psum:
-            old = in_psum
-            new = waiting[:GROUPS_A_STEP]
+        while step <= len(CHUNKS) or waiting:
+            for group in waiting[:GROUPS_A_STEP]:
+                multiply(group)
+                in_psum.append(group)
+                if len(in_psum) > LAG:
+                    finish(in_psum.pop(0))
             waiting = waiting[GROUPS_A_STEP:]
-            in_psum = new
-            for i in range(max(len(old), len(new))):
-                if i < len(old):
-                    finish(old[i])
-                if i < len(new):
-                    multiply(new[i])
+            if not waiting:
+                for group in in_psum:
+                    finish(group)
+                in_psum = []
+            if step < len(CHUNKS):
+                interleave(CHUNKS[step])
             if 1 <= step <= len(CHUNKS):
                 quantize(CHUNKS[step - 1])
                 done.add(CHUNKS[step - 1])
                 waiting = sorted(waiting + newly_ready())
-            if step < len(CHUNKS):
-                interleave(CHUNKS[step])
             step += 1

from contextlib import ExitStack

import concourse.mybir as mybir
from concourse.masks import make_identity

K, M, T = 512, 1536, 2048
FLOPS = 2 * 2 * K * M * T

F32 = mybir.dt.float32
BF16 = mybir.dt.bfloat16
U32 = mybir.dt.uint32
U8 = mybir.dt.uint8
E4M3 = mybir.dt.float8_e4m3fn_x4
E5M2 = mybir.dt.float8_e5m2_x4
ADD = mybir.AluOpType.add

P = 128
PACK = 4
CHUNK = 512
N_TILES = M // CHUNK

FORMAT = {"w": E4M3, "x": E4M3, "xd": E5M2, "wd": E5M2}
WIDTH = {"w": M, "wd": M, "x": T, "xd": T}

LOADS = [
    ("w", 0, 1024),
    ("wd", 0, 1024),
    ("x", 0, 512),
    ("xd", 0, 512),
    ("w", 1024, 512),
    ("wd", 1024, 512),
    ("x", 512, 512),
    ("xd", 512, 512),
    ("xd", 1024, 1024),
    ("x", 1024, 1024),
]
CHUNKS = [
    ("w", 0),
    ("w", 512),
    ("wd", 0),
    ("wd", 512),
    ("x", 0),
    ("xd", 0),
    ("w", 1024),
    ("wd", 1024),
    ("x", 512),
    ("xd", 512),
    ("xd", 1024),
    ("xd", 1536),
    ("x", 1024),
    ("x", 1536),
]
ON_VECTOR = {("w", 0), ("wd", 0), ("xd", 0)}
GROUPS_A_STEP = 8
PAIR = 2
FIRST_SPLIT = 5
LAG = 2


def tile_mix_jvp_tm_bias_kernel(tc, w, xd, wd, x, b, out):
    nc = tc.nc
    dram = {"w": w, "xd": xd, "wd": wd, "x": x}

    with ExitStack() as ctx:
        keep = ctx.enter_context(tc.tile_pool(name="keep", bufs=1))
        stage = ctx.enter_context(tc.tile_pool(name="stage", bufs=4))
        results = ctx.enter_context(tc.tile_pool(name="results", bufs=5))
        psum = ctx.enter_context(tc.psum_pool(name="psum", bufs=8))
        ctx.enter_context(tc.manual_schedule())

        codes = {}
        scales = {}
        for key in WIDTH:
            codes[key] = keep.tile([P, WIDTH[key]], U32, align_bytes=64, name="codes_" + key)
            scales[key] = keep.tile([P, WIDTH[key]], U8, align_bytes=64, name="scales_" + key)

        per_part = M // P
        b_cols = keep.tile([P, per_part], F32, name="b_cols")
        nc.scalar.dma_start(out=b_cols[:], in_=b.rearrange("(p c) -> p c", c=per_part))

        source = {}
        for key, first, cols in LOADS:
            raw = keep.tile([P, PACK, cols], F32, name="raw_%s_%d" % (key, first))
            nc.sync.dma_start(
                out=raw[:],
                in_=dram[key].rearrange("(p j) c -> p j c", j=PACK)[:, :, first : first + cols],
            )
            for c0 in range(0, cols, CHUNK):
                source[(key, first + c0)] = raw[:, :, c0 : c0 + CHUNK]

        identity = keep.tile([P, P], F32, name="identity")
        make_identity(nc, identity[:])
        bias = keep.tile([P, M], F32, name="bias")

        def spread_bias():
            for g in range(per_part // 4):
                bank = psum.tile([P, CHUNK], F32, name="acc")
                for i in range(4):
                    c = 4 * g + i
                    nc.tensor.transpose(
                        bank[:, i * P : (i + 1) * P],
                        b_cols[:, c : c + 1].to_broadcast([P, P]),
                        identity[:],
                    )
                nc.scalar.copy(
                    out=bias[:].rearrange("p (q c) -> p q c", c=per_part)[:, :, 4 * g : 4 * g + 4],
                    in_=bank[:].rearrange("p (c q) -> p q c", c=4),
                )

        spread_bias()

        grouped = {}

        def interleave(chunk):
            tile = stage.tile([P, CHUNK, PACK], BF16, align_bytes=64, name="grouped")
            grouped[chunk] = tile
            view = source[chunk].rearrange("p j c -> p c j")
            if chunk in ON_VECTOR:
                nc.vector.tensor_copy(out=tile[:], in_=view)
            else:
                nc.scalar.copy(out=tile[:], in_=view)

        def quantize(chunk):
            key, first = chunk
            cols = slice(first, first + CHUNK)
            nc.vector.quantize_mx(
                out=codes[key][:, cols].bitcast(FORMAT[key]),
                scales=scales[key][:, cols],
                in_=grouped[chunk][:].rearrange("p c j -> p (c j)"),
            )

        banks = {}
        rows = {}

        def multiply(group):
            pair, s, n = group
            t_first = (pair * PAIR + s) * P
            t_cols = slice(t_first, t_first + P)
            n_cols = slice(n * CHUNK, (n + 1) * CHUNK)
            acc = psum.tile([P, CHUNK], F32, name="acc")
            banks[group] = acc
            for still, moving in (("xd", "w"), ("x", "wd")):
                nc.tensor.matmul_mx(
                    out=acc[:],
                    lhsT=codes[still][:, t_cols].bitcast(FORMAT[still]),
                    lhsT_scale=scales[still][:, t_cols],
                    rhs=codes[moving][:, n_cols].bitcast(FORMAT[moving]),
                    rhs_scale=scales[moving][:, n_cols],
                    start=(still == "xd"),
                    stop=(still == "x"),
                )

        def finish(group):
            pair, s, n = group
            n_cols = slice(n * CHUNK, (n + 1) * CHUNK)
            if pair not in rows:
                row = results.tile([P, PAIR, M], F32, name="row")
                rows[pair] = row
            nc.vector.tensor_tensor(
                out=rows[pair][:, s, n_cols], in0=banks[group][:], in1=bias[:, n_cols], op=ADD
            )
            if n == N_TILES - 1:
                target = out[pair * PAIR * P : (pair + 1) * PAIR * P, :].rearrange("(s m) c -> m s c", s=PAIR)
                if pair >= FIRST_SPLIT:
                    queue = nc.scalar if s == PAIR - 1 else nc.sync
                    queue.dma_start(out=target[:, s, :], in_=rows[pair][:, s, :])
                elif s == PAIR - 1:
                    queue = nc.scalar if pair == FIRST_SPLIT - 1 else nc.sync
                    queue.dma_start(out=target, in_=rows[pair][:])

        done = set()
        issued = set()

        def newly_ready():
            ready = []
            for pair in range(T // (PAIR * P)):
                for s in range(PAIR):
                    for n in range(N_TILES):
                        t_first = (pair // 2) * CHUNK
                        need = [("xd", t_first), ("x", t_first), ("w", n * CHUNK), ("wd", n * CHUNK)]
                        if all([c in done for c in need]) and (pair, s, n) not in issued:
                            ready.append((pair, s, n))
                            issued.add((pair, s, n))
            return ready

        waiting = []
        in_psum = []
        step = 0
        while step <= len(CHUNKS) or waiting:
            for group in waiting[:GROUPS_A_STEP]:
                multiply(group)
                in_psum.append(group)
                if len(in_psum) > LAG:
                    finish(in_psum.pop(0))
            waiting = waiting[GROUPS_A_STEP:]
            if not waiting:
                for group in in_psum:
                    finish(group)
                in_psum = []
            if step < len(CHUNKS):
                interleave(CHUNKS[step])
            if 1 <= step <= len(CHUNKS):
                quantize(CHUNKS[step - 1])
                done.add(CHUNKS[step - 1])
                waiting = sorted(waiting + newly_ready())
            step += 1
